import numpy as np
import ml_dtypes


def mxq(x, axis, fmt="e4m3"):
    dtype, down = {"e4m3": (ml_dtypes.float8_e4m3fn, 7), "e5m2": (ml_dtypes.float8_e5m2, 14)}[fmt]
    v = np.moveaxis(np.asarray(x, np.float32).astype(ml_dtypes.bfloat16).astype(np.float64), axis, -1)
    blocks = v.reshape(v.shape[:-1] + (-1, 32))
    amax = np.abs(blocks).max(-1, keepdims=True)
    byte = np.maximum(np.where(amax > 0, np.frexp(amax)[1] - 1 + 127, 0) - down, 1)
    scale = np.exp2(byte - 127.0)
    codes = (blocks / scale).astype(np.float32).astype(dtype).astype(np.float64)
    return np.moveaxis((codes * scale).reshape(v.shape), -1, axis)


WIDE = False


def mx_kscale(k):
    if not WIDE:
        return np.ones(k)
    levels = np.array([30, -30])
    if k % 512:
        return np.exp2(np.random.permutation(np.resize(levels, k // 32))).repeat(32)
    a = np.empty((k // 512, 16))
    for p in range(k // 512):
        a[p, :8] = np.random.permutation(np.resize(levels, 8))
        for g in range(8):
            far = levels[np.abs(levels - a[p, g]) >= 10]
            a[p, g + 8] = far[np.random.randint(len(far))]
    return np.exp2(a.ravel()).repeat(32)


def f64(x):
    return np.asarray(x).astype(np.float64)


def striped(idx):
    return np.tile(np.asarray(idx).reshape(-1, 16).T, (8, 1)).astype(np.uint16)


def unstriped(offs):
    return offs[:16].T.reshape(-1).astype(np.int64)


E2M1 = np.array([0.0, 0.5, 1.0, 1.5, 2.0, 3.0, 4.0, 6.0, -0.0, -0.5, -1.0, -1.5, -2.0, -3.0, -4.0, -6.0])


def pack_weight(w, fmt):
    k, n = w.shape
    w = f64(np.asarray(w, np.float32).astype(ml_dtypes.bfloat16)).reshape(k // 32, 32, n)
    amax = np.abs(w).max(1)
    if fmt in ("e4m3", "e5m2"):
        byte = np.frexp(amax)[1] - 1 + 127 - (7 if fmt == "e4m3" else 14)
    else:
        mant, ex = np.frexp(amax / 6.0)
        byte = np.where(mant > 0.5, ex, ex - 1) + 127
    byte = np.clip(np.where(amax > 0, byte, 1), 1, 254)
    scaled = (w * np.exp2(127.0 - byte)[:, None, :]).reshape(k, n).astype(np.float32)
    by_word = np.ascontiguousarray(scaled.reshape(k // 512, 128, 4, n).transpose(0, 1, 3, 2))
    if fmt in ("e4m3", "e5m2"):
        words = by_word.astype(ml_dtypes.float8_e4m3fn if fmt == "e4m3" else ml_dtypes.float8_e5m2).view(np.uint8)
    else:
        c = by_word.astype(ml_dtypes.float4_e2m1fn).view(np.uint8) & 0xF
        words = (c[..., 0::2] | (c[..., 1::2] << 4)).reshape(k // 512, 128, 2 * n)
    return np.ascontiguousarray(words), np.ascontiguousarray(byte.astype(np.uint8).reshape(k // 512, 16, n))


def unpack_weight(words, scales, fmt):
    g, _, n = scales.shape
    words = np.ascontiguousarray(words).reshape(g, 128, n, -1)
    if fmt in ("e4m3", "e5m2"):
        vals = words.view(ml_dtypes.float8_e4m3fn if fmt == "e4m3" else ml_dtypes.float8_e5m2).astype(np.float64)
    else:
        nib = np.empty((g, 128, n, 4), np.uint8)
        nib[..., 0::2] = words & 0xF
        nib[..., 1::2] = words >> 4
        vals = E2M1[nib]
    vals = vals * np.repeat(np.exp2(scales.astype(np.float64) - 127.0), 8, axis=1)[..., None]
    return vals.transpose(0, 1, 3, 2).reshape(g * 512, n)


K, T, J, N, E = 512, 1024, 256, 256, 512


def setup_inputs():
    n = np.random.standard_normal
    idx = np.random.permutation(T)[:J]
    idx2 = np.random.permutation(E)[:J]
    fk = mx_kscale(K)
    wp = pack_weight(n((K, N)) * 1 / np.sqrt(K) / fk[:, None], "e2m1")
    wdp = pack_weight((np.random.uniform(0.4, 2.0, (K, N)) / K) / fk[:, None], "e5m2")
    return {
        "ca": (np.random.randint(1, 10, (K, T)).astype(np.float64) ** 2).astype(np.float32),
        "sa": (np.random.uniform(0.1, 0.4, (K, 1)) * fk[:, None]).astype(np.float32),
        "w_words": wp[0],
        "w_scales": wp[1],
        "wd_words": wdp[0],
        "wd_scales": wdp[1],
        "so": (np.random.uniform(0.5, 1.6, (N, 1))).astype(np.float32),
        "offs": striped(idx),
        "offs2": striped(idx2),
    }


def reference(ca, sa, w_words, w_scales, wd_words, wd_scales, so, offs, offs2):
    idx = unstriped(offs)
    idx2 = unstriped(offs2)
    wu = unpack_weight(w_words, w_scales, "e2m1")
    wdu = unpack_weight(wd_words, wd_scales, "e5m2")
    z = f64(ca)[:, idx] * f64(sa)
    zq = mxq(z, 0, "e4m3")
    p = wu.T @ zq
    d = wdu.T @ zq
    m0 = p / d
    y = np.zeros((N, E))
    y[:, idx2] = m0 * f64(so)
    return y

@@ -1,0 +1,143 @@
+from contextlib import ExitStack
+
+import concourse.mybir as mybir
+
+K, T, J, N, E = 512, 1024, 256, 256, 512
+FLOPS = 2 * 2 * K * N * J
+
+F32 = mybir.dt.float32
+BF16 = mybir.dt.bfloat16
+I32 = mybir.dt.int32
+U32 = mybir.dt.uint32
+U16 = mybir.dt.uint16
+U8 = mybir.dt.uint8
+E4M3 = mybir.dt.float8_e4m3fn_x4
+E5M2 = mybir.dt.float8_e5m2_x4
+E2M1 = mybir.dt.float4_e2m1fn_x4
+ACT = mybir.ActivationFunctionType
+ALU = mybir.AluOpType
+
+P = 128
+PACK = 4
+CHUNK = 128
+HALVES = N // P
+CHUNKS = J // CHUNK
+LIST_COLS = CHUNK // 16
+
+
+def tile_list_codedshare_kernel(tc, ca, sa, w_words, w_scales, wd_words, wd_scales, so, offs, offs2, out):
+    nc = tc.nc
+    with ExitStack() as ctx:
+        sb = ctx.enter_context(tc.tile_pool(name="sb", bufs=1))
+        ps = ctx.enter_context(tc.psum_pool(name="ps", bufs=1))
+
+        idx = sb.tile([P, J // 16], U16, name="idx")
+        idx2 = sb.tile([P, J // 16], U16, name="idx2")
+        counts = [sb.tile([P, T], F32, name=f"counts{r}") for r in range(PACK)]
+        unit = sb.tile([P, PACK], F32, name="unit")
+        weight = sb.tile([P, HALVES], F32, name="weight")
+        w_codes = sb.tile([P, 2 * N], U8, name="w_codes", align_bytes=64)
+        wd_codes = sb.tile([P, N], U32, name="wd_codes", align_bytes=64)
+        w_stage = sb.tile([4, 4, N // 4], I32, name="w_stage")
+        wd_stage = sb.tile([4, 4, N // 4], I32, name="wd_stage")
+        w_plane = sb.tile([P, N], U8, name="w_plane", align_bytes=64)
+        wd_plane = sb.tile([P, N], U8, name="wd_plane", align_bytes=64)
+        pages = [sb.tile([P, E], F32, name=f"page{h}") for h in range(HALVES)]
+
+        ca_rows = ca.rearrange("(p r) t -> r p t", r=PACK)
+        nc.sync.dma_start(out=counts[0][:], in_=ca_rows[0])
+        nc.sync.dma_start(idx[:], offs)
+        nc.sync.dma_start(out=unit[:], in_=sa.rearrange("(p r) o -> p (r o)", r=PACK))
+        nc.sync.dma_start(out=wd_stage[:], in_=wd_scales[0].bitcast(I32).rearrange("(q r) c -> r q c", r=4))
+        nc.sync.dma_start(out=w_stage[:], in_=w_scales[0].bitcast(I32).rearrange("(q r) c -> r q c", r=4))
+        for r in range(1, PACK):
+            nc.sync.dma_start(out=counts[r][:], in_=ca_rows[r])
+        nc.sync.dma_start(out=wd_codes[:].bitcast(I32), in_=wd_words[0].rearrange("p n t -> p (n t)").bitcast(I32))
+        nc.sync.dma_start(out=w_codes[:].bitcast(I32), in_=w_words[0].bitcast(I32))
+        nc.sync.dma_start(idx2[:], offs2)
+        with nc.allow_non_contiguous_dma(reason="one float32 weight for each partition and half"):
+            nc.sync.dma_start(out=weight[:], in_=so.rearrange("(h p) o -> p (h o)", p=P))
+
+        for stage, plane in ((wd_stage, wd_plane), (w_stage, w_plane)):
+            nc.vector.memset(plane[:].bitcast(I32), 0)
+        for h in range(HALVES):
+            nc.vector.memset(pages[h][:], 0.0)
+        for stage, plane in ((wd_stage, wd_plane), (w_stage, w_plane)):
+            for q in range(4):
+                nc.vector.tensor_copy(out=plane[32 * q : 32 * q + 4, :].bitcast(I32), in_=stage[:, q, :])
+
+        z = [sb.tile([P, PACK * CHUNK], BF16, name=f"z{c}", align_bytes=64) for c in range(CHUNKS)]
+        for r in range(PACK):
+            for c in range(CHUNKS):
+                nc.scalar.activation(
+                    out=z[c][:, r : PACK * CHUNK : PACK],
+                    in_=counts[r][:].indirect(idx[:, c * LIST_COLS : (c + 1) * LIST_COLS]),
+                    func=ACT.Copy,
+                    scale=unit[:, r : r + 1],
+                )
+
+        z_codes = [sb.tile([P, CHUNK], U32, name=f"z_codes{c}", align_bytes=64) for c in range(CHUNKS)]
+        z_plane = [sb.tile([P, CHUNK], U8, name=f"z_plane{c}", align_bytes=64) for c in range(CHUNKS)]
+        for c in range(CHUNKS):
+            nc.vector.quantize_mx(out=z_codes[c][:].bitcast(E4M3), scales=z_plane[c][:], in_=z[c][:])
+
+        pieces = [(c, h) for c in range(CHUNKS) for h in range(HALVES)]
+        den = {}
+        num = {}
+
+        def product(c, h, is_den):
+            cols = slice(P * h, P * (h + 1))
+            acc = ps.tile([P, CHUNK], F32, name=f"acc{c}{h}{int(is_den)}")
+            if is_den:
+                lhsT, scale = wd_codes[:, cols].bitcast(E5M2), wd_plane[:, cols]
+                den[(c, h)] = acc
+            else:
+                lhsT, scale = w_codes[:, 2 * P * h : 2 * P * (h + 1)].bitcast(E2M1), w_plane[:, cols]
+                num[(c, h)] = acc
+            nc.tensor.matmul_mx(
+                out=acc[:], lhsT=lhsT, lhsT_scale=scale,
+                rhs=z_codes[c][:].bitcast(E4M3), rhs_scale=z_plane[c][:], start=True, stop=True,
+            )
+
+        product(0, 0, True)
+        product(0, 0, False)
+        for c, h in pieces[1:]:
+            product(c, h, True)
+        for c, h in pieces[1:]:
+            product(c, h, False)
+
+        root = {}
+        sign = {}
+        for c, h in pieces:
+            root[(c, h)] = sb.tile([P, CHUNK], F32, name=f"root{c}{h}")
+            sign[(c, h)] = sb.tile([P, CHUNK], F32, name=f"sign{c}{h}")
+            nc.scalar.activation(out=root[(c, h)][:], in_=den[(c, h)][:], func=ACT.Abs_reciprocal_sqrt)
+            if (c, h) == (0, 0):
+                nc.scalar.activation(out=sign[(c, h)][:], in_=den[(c, h)][:], func=ACT.Sign, scale=1.0)
+
+        for c, h in pieces:
+            left = sb.tile([P, CHUNK], F32, name=f"left{c}{h}")
+            right = sb.tile([P, CHUNK], F32, name=f"right{c}{h}")
+            quot = sb.tile([P, CHUNK], F32, name=f"quot{c}{h}")
+            if (c, h) == (0, 0):
+                nc.vector.tensor_tensor(out=left[:], in0=num[(c, h)][:], in1=root[(c, h)][:], op=ALU.mult)
+                nc.vector.tensor_tensor(out=right[:], in0=sign[(c, h)][:], in1=root[(c, h)][:], op=ALU.mult)
+            else:
+                nc.vector.tensor_scalar(
+                    out=sign[(c, h)][:], in0=den[(c, h)][:], scalar1=0.0, scalar2=0.5,
+                    op0=ALU.is_ge, op1=ALU.subtract,
+                )
+                nc.vector.tensor_tensor(out=left[:], in0=num[(c, h)][:], in1=root[(c, h)][:], op=ALU.mult)
+                nc.vector.scalar_tensor_tensor(
+                    out=right[:], in0=sign[(c, h)][:], scalar=2.0, in1=root[(c, h)][:],
+                    op0=ALU.mult, op1=ALU.mult,
+                )
+            nc.vector.tensor_tensor(out=quot[:], in0=left[:], in1=right[:], op=ALU.mult)
+            nc.scalar.activation(
+                out=pages[h][:].indirect(idx2[:, c * LIST_COLS : (c + 1) * LIST_COLS]),
+                in_=quot[:],
+                func=ACT.Copy,
+                scale=weight[:, h : h + 1],
+            )
+        for h in range(HALVES):
+            nc.sync.dma_start(out=out[P * h : P * (h + 1), :], in_=pages[h][:])

@@ -44,6 +44,11 @@ def tile_list_codedshare_kernel(tc, ca, sa, w_words, w_scales, wd_words, wd_scal
         wd_plane = sb.tile([P, N], U8, name="wd_plane", align_bytes=64)
         pages = [sb.tile([P, E], F32, name=f"page{h}") for h in range(HALVES)]
 
+        ones = sb.tile([P, 1], F32, name="ones")
+        warm = sb.tile([P, 1], F32, name="warm")
+        nc.vector.memset(ones[:], 1.0)
+        nc.scalar.activation(out=warm[:], in_=ones[:], func=ACT.Abs_reciprocal_sqrt)
+
         ca_rows = ca.rearrange("(p r) t -> r p t", r=PACK)
         nc.sync.dma_start(out=counts[0][:], in_=ca_rows[0])
         nc.sync.dma_start(idx[:], offs)

from contextlib import ExitStack

import concourse.mybir as mybir

K, T, J, N, E = 512, 1024, 256, 256, 512
FLOPS = 2 * 2 * K * N * J

F32 = mybir.dt.float32
BF16 = mybir.dt.bfloat16
I32 = mybir.dt.int32
U32 = mybir.dt.uint32
U16 = mybir.dt.uint16
U8 = mybir.dt.uint8
E4M3 = mybir.dt.float8_e4m3fn_x4
E5M2 = mybir.dt.float8_e5m2_x4
E2M1 = mybir.dt.float4_e2m1fn_x4
ACT = mybir.ActivationFunctionType
ALU = mybir.AluOpType

P = 128
PACK = 4
CHUNK = 128
HALVES = N // P
CHUNKS = J // CHUNK
LIST_COLS = CHUNK // 16


def tile_list_codedshare_kernel(tc, ca, sa, w_words, w_scales, wd_words, wd_scales, so, offs, offs2, out):
    nc = tc.nc
    with ExitStack() as ctx:
        sb = ctx.enter_context(tc.tile_pool(name="sb", bufs=1))
        ps = ctx.enter_context(tc.psum_pool(name="ps", bufs=1))

        idx = sb.tile([P, J // 16], U16, name="idx")
        idx2 = sb.tile([P, J // 16], U16, name="idx2")
        counts = [sb.tile([P, T], F32, name=f"counts{r}") for r in range(PACK)]
        unit = sb.tile([P, PACK], F32, name="unit")
        weight = sb.tile([P, HALVES], F32, name="weight")
        w_codes = sb.tile([P, 2 * N], U8, name="w_codes", align_bytes=64)
        wd_codes = sb.tile([P, N], U32, name="wd_codes", align_bytes=64)
        w_stage = sb.tile([4, 4, N // 4], I32, name="w_stage")
        wd_stage = sb.tile([4, 4, N // 4], I32, name="wd_stage")
        w_plane = sb.tile([P, N], U8, name="w_plane", align_bytes=64)
        wd_plane = sb.tile([P, N], U8, name="wd_plane", align_bytes=64)
        pages = [sb.tile([P, E], F32, name=f"page{h}") for h in range(HALVES)]

        ones = sb.tile([P, 1], F32, name="ones")
        warm = sb.tile([P, 1], F32, name="warm")
        nc.vector.memset(ones[:], 1.0)
        nc.scalar.activation(out=warm[:], in_=ones[:], func=ACT.Abs_reciprocal_sqrt)

        ca_rows = ca.rearrange("(p r) t -> r p t", r=PACK)
        nc.sync.dma_start(out=counts[0][:], in_=ca_rows[0])
        nc.sync.dma_start(idx[:], offs)
        nc.sync.dma_start(out=unit[:], in_=sa.rearrange("(p r) o -> p (r o)", r=PACK))
        nc.sync.dma_start(out=wd_stage[:], in_=wd_scales[0].bitcast(I32).rearrange("(q r) c -> r q c", r=4))
        nc.sync.dma_start(out=w_stage[:], in_=w_scales[0].bitcast(I32).rearrange("(q r) c -> r q c", r=4))
        for r in range(1, PACK):
            nc.sync.dma_start(out=counts[r][:], in_=ca_rows[r])
        nc.sync.dma_start(out=wd_codes[:].bitcast(I32), in_=wd_words[0].rearrange("p n t -> p (n t)").bitcast(I32))
        nc.sync.dma_start(out=w_codes[:].bitcast(I32), in_=w_words[0].bitcast(I32))
        nc.sync.dma_start(idx2[:], offs2)
        with nc.allow_non_contiguous_dma(reason="one float32 weight for each partition and half"):
            nc.sync.dma_start(out=weight[:], in_=so.rearrange("(h p) o -> p (h o)", p=P))

        for stage, plane in ((wd_stage, wd_plane), (w_stage, w_plane)):
            nc.vector.memset(plane[:].bitcast(I32), 0)
        for h in range(HALVES):
            nc.vector.memset(pages[h][:], 0.0)
        for stage, plane in ((wd_stage, wd_plane), (w_stage, w_plane)):
            for q in range(4):
                nc.vector.tensor_copy(out=plane[32 * q : 32 * q + 4, :].bitcast(I32), in_=stage[:, q, :])

        z = [sb.tile([P, PACK * CHUNK], BF16, name=f"z{c}", align_bytes=64) for c in range(CHUNKS)]
        for r in range(PACK):
            for c in range(CHUNKS):
                nc.scalar.activation(
                    out=z[c][:, r : PACK * CHUNK : PACK],
                    in_=counts[r][:].indirect(idx[:, c * LIST_COLS : (c + 1) * LIST_COLS]),
                    func=ACT.Copy,
                    scale=unit[:, r : r + 1],
                )

        z_codes = [sb.tile([P, CHUNK], U32, name=f"z_codes{c}", align_bytes=64) for c in range(CHUNKS)]
        z_plane = [sb.tile([P, CHUNK], U8, name=f"z_plane{c}", align_bytes=64) for c in range(CHUNKS)]
        for c in range(CHUNKS):
            nc.vector.quantize_mx(out=z_codes[c][:].bitcast(E4M3), scales=z_plane[c][:], in_=z[c][:])

        pieces = [(c, h) for c in range(CHUNKS) for h in range(HALVES)]
        den = {}
        num = {}

        def product(c, h, is_den):
            cols = slice(P * h, P * (h + 1))
            acc = ps.tile([P, CHUNK], F32, name=f"acc{c}{h}{int(is_den)}")
            if is_den:
                lhsT, scale = wd_codes[:, cols].bitcast(E5M2), wd_plane[:, cols]
                den[(c, h)] = acc
            else:
                lhsT, scale = w_codes[:, 2 * P * h : 2 * P * (h + 1)].bitcast(E2M1), w_plane[:, cols]
                num[(c, h)] = acc
            nc.tensor.matmul_mx(
                out=acc[:], lhsT=lhsT, lhsT_scale=scale,
                rhs=z_codes[c][:].bitcast(E4M3), rhs_scale=z_plane[c][:], start=True, stop=True,
            )

        product(0, 0, True)
        product(0, 0, False)
        for c, h in pieces[1:]:
            product(c, h, True)
        for c, h in pieces[1:]:
            product(c, h, False)

        root = {}
        sign = {}
        for c, h in pieces:
            root[(c, h)] = sb.tile([P, CHUNK], F32, name=f"root{c}{h}")
            sign[(c, h)] = sb.tile([P, CHUNK], F32, name=f"sign{c}{h}")
            nc.scalar.activation(out=root[(c, h)][:], in_=den[(c, h)][:], func=ACT.Abs_reciprocal_sqrt)
            if (c, h) == (0, 0):
                nc.scalar.activation(out=sign[(c, h)][:], in_=den[(c, h)][:], func=ACT.Sign, scale=1.0)

        for c, h in pieces:
            left = sb.tile([P, CHUNK], F32, name=f"left{c}{h}")
            right = sb.tile([P, CHUNK], F32, name=f"right{c}{h}")
            quot = sb.tile([P, CHUNK], F32, name=f"quot{c}{h}")
            if (c, h) == (0, 0):
                nc.vector.tensor_tensor(out=left[:], in0=num[(c, h)][:], in1=root[(c, h)][:], op=ALU.mult)
                nc.vector.tensor_tensor(out=right[:], in0=sign[(c, h)][:], in1=root[(c, h)][:], op=ALU.mult)
            else:
                nc.vector.tensor_scalar(
                    out=sign[(c, h)][:], in0=den[(c, h)][:], scalar1=0.0, scalar2=0.5,
                    op0=ALU.is_ge, op1=ALU.subtract,
                )
                nc.vector.tensor_tensor(out=left[:], in0=num[(c, h)][:], in1=root[(c, h)][:], op=ALU.mult)
                nc.vector.scalar_tensor_tensor(
                    out=right[:], in0=sign[(c, h)][:], scalar=2.0, in1=root[(c, h)][:],
                    op0=ALU.mult, op1=ALU.mult,
                )
            nc.vector.tensor_tensor(out=quot[:], in0=left[:], in1=right[:], op=ALU.mult)
            nc.scalar.activation(
                out=pages[h][:].indirect(idx2[:, c * LIST_COLS : (c + 1) * LIST_COLS]),
                in_=quot[:],
                func=ACT.Copy,
                scale=weight[:, h : h + 1],
            )
        for h in range(HALVES):
            nc.sync.dma_start(out=out[P * h : P * (h + 1), :], in_=pages[h][:])
